import numpy as np, ml_dtypes
CORES = [24,25,26,27,28,29,30,31]
N = 8
BF = ml_dtypes.bfloat16
V, HB, KB, S, SB, M, CL, RO = 4096, 11, 2048, 112, 16, 2, 16, 3
def hashes(v, a, t):
    u = np.matmul(a.transpose(0, 1, 3, 2), v)
    return np.add.reduce((u > t[..., None]) * (2 ** np.arange(HB))[:, None], axis=2)
def parts(rng):
    a = rng.integers(-8, 9, (1, 8, 16, HB))
    t = np.rint(127.5 * np.add.reduce(a, axis=2) + 700 * rng.standard_normal((1, 8, HB))).astype(np.int64)
    x = rng.integers(0, 256, (N, 8, 16, V)); s = rng.integers(0, 256, (N, 8, 16, S)); b = rng.integers(0, V, (N, 8, 16, KB))
    return x, s, b, a, t
def near(rng, x, s, b, a, t, d, share, twins):
    m = rng.integers(0, V, (N, 8, S)); p = np.take_along_axis(x, m[:, :, None, :], 3)
    v = np.where(rng.random((N, 8, 1, S)) < share, np.clip(p + d, 0, 255), s)
    for q in range(N):
        for g in range(8):
            o = rng.permutation(S); v[q, g][:, o[:twins]] = v[q, g][:, o[twins:2 * twins]]; m[q, g, o[:twins]] = m[q, g, o[twins:2 * twins]]
    b[np.arange(N)[:, None, None], np.arange(8)[None, :, None], rng.integers(0, 16, (N, 8, S)), hashes(v, a, t)] = m
    return v
def pack(x, s, b, a, t):
    w = np.zeros((N, 8, 16, 16), np.float32); w[..., :HB] = a
    z = np.zeros((N, 8, 16), np.int32); z[..., :HB] = t
    return {"nx": x.reshape(N, 128, V).astype(np.float32).astype(BF), "bk": np.ascontiguousarray(b.reshape(N, 128, KB)).astype(np.int32),
            "s0": s.reshape(N, 128, S).astype(np.float32).astype(BF), "pa": w.reshape(N, 128, 16).astype(BF), "th": z.reshape(N, 128, 1)}
def setup_inputs(rng):
    x, s, b, a, t = parts(rng)
    s = near(rng, x, s, b, a, t, rng.integers(-40, 41, s.shape), 0.5, S // 8)
    return pack(x, s, b, a, t)
def setup_inputs_ties(rng):
    x, s, b, a, t = parts(rng)
    pat = rng.integers(0, 256, (N, 8, 16, 24)); x = np.take_along_axis(pat, rng.integers(0, 24, (N, 8, 1, V)), 3)
    s = np.where(rng.random((N, 8, 1, S)) < 0.5, np.take_along_axis(pat, rng.integers(0, 24, (N, 8, 1, S)), 3), s)
    for i in range(HB): t[0, :, i] = np.add.reduce(a[0, :, :, i] * s[i % N, :, :, (7 * i) % S], axis=1)
    return pack(x, s, b, a, t)
def setup_inputs_alike(rng):
    x, s, b, a, t = parts(rng)
    s[:, 0] = s[:, 0, :, :1].copy(); s[:, 1] = np.repeat(s[:, 1, :, :S // 16], 16, axis=2)
    b[:, 2] = rng.choice(np.array([0, 1, V - 2, V - 1]), (N, 16, KB)); t[:, 3] = 32767; t[:, 4] = -32768
    b[:, 5] = b[:, 5, :1].copy(); b[:, 6, :, 1::2] = b[:, 6, :, 0::2]
    t[:, 7] = 32767
    for q in range(N):
        m = 16 * rng.integers(0, V // 16, 2); lo, hi = int(m[0]), int(m[1]) + 8
        x[q, 7][:, lo] = rng.integers(0, 4, 16); x[q, 7][:, hi] = rng.integers(252, 256, 16)
        b[q, 7, :, :M] = hi; b[q, 7, 0, :M] = lo
    s[:, 7] = rng.integers(0, 4, (N, 16, S)); s[:, 7, :, :2] = 255 - s[:, 7, :, :2]
    return pack(x, s, b, a, t)
def setup_inputs_ends(rng):
    x, s, b, a, t = parts(rng)
    x = rng.integers(CL + 1, 255 - CL, x.shape); d = rng.choice(np.array([-CL - 1, -CL, 1 - CL, -1, 0, 1, CL - 1, CL, CL + 1]), s.shape)
    s = near(rng, x, s, b, a, t, d, 0.9, 2)
    x[:, 5] = 255 * rng.integers(0, 2, (N, 16, V)); s[:, 5] = 255 * rng.integers(0, 2, (N, 16, S)); x[:, 6] = 255; s[:, 6] = 0
    e = HB - 1; a[0, 3] = np.eye(16, HB, dtype=np.int64)
    t[0, 3] = CL // 2; t[0, 3, 1::2] = 0; t[0, 3, e] = 2 * CL + CL // 2
    pat = rng.permutation(2 ** e)[:S] + 2 ** e
    on = np.ones((16, S), bool); on[:HB] = ((pat[None, :] >> np.arange(HB)[:, None]) & 1) == 1
    s[:, 3] = np.where(on, rng.integers(128, 161, (N, 16, S)), 0); x[:, 3] = 0
    for q in range(N): b[q, 3, 0, pat] = rng.permutation(V)[:S]
    a[0, 4] = np.where(np.arange(HB) % 2 == 1, -1, 1) * (8 - (rng.random((16, HB)) < 0.125).astype(np.int64))
    a[0, 4, :, 0] = 8; a[0, 4, :, 1] = -8
    t[0, 4] = np.clip(240 * np.add.reduce(a[0, 4], axis=0) + np.rint(250 * rng.standard_normal(HB)).astype(np.int64), -32768, 32767)
    t[0, 4, 0] = 32639; t[0, 4, 1] = -32640
    x[:, 4] = rng.integers(225, 256, (N, 16, V)); s[:, 4] = rng.integers(225, 256, (N, 16, S)); s[:, 4, :, ::8] = 255
    x[:, 7] = rng.integers(253, 256, (N, 16, V)); s[:, 7] = rng.integers(0, 41, (N, 16, S))
    t[0, 7] = np.rint(20 * np.add.reduce(a[0, 7], axis=0) + 100 * rng.standard_normal(HB)).astype(np.int64)
    return pack(x, s, b, a, t)
def setup_inputs_few(rng):
    x, s, b, a, t = parts(rng)
    t[:, :, 5:] = np.where(rng.random((1, 8, HB - 5)) < 0.5, 32767, -32768)
    a[:, 1, :, 6] = 0; t[:, 1, 6] = -1; a[:, 2, :, 7] = 0; t[:, 2, 7] = 0
    s = near(rng, x, s, b, a, t, rng.integers(-60, 61, s.shape), 0.7, S // 8)
    return pack(x, s, b, a, t)
def setup_inputs_spread(rng):
    x, s, b, a, t = parts(rng)
    a = np.where(rng.random(a.shape) < 0.5, 0, a)
    t = np.rint(40 * np.add.reduce(a, axis=2) + 400 * rng.standard_normal((1, 8, HB))).astype(np.int64)
    x = np.minimum((np.exp2(8 * rng.random((N, 8, 1, V))) * rng.random(x.shape)).astype(np.int64), 255)
    s = np.minimum((np.exp2(8 * rng.random((N, 8, 1, S))) * rng.random(s.shape)).astype(np.int64), 255)
    b = np.minimum((V * rng.random(b.shape) ** 3).astype(np.int64), V - 1)
    return pack(x, s, b, a, t)
def check_inputs(d):
    bad = []
    for k, lo, hi in (("nx", 0, 255), ("bk", 0, V - 1), ("s0", 0, 255), ("pa", -8, 8), ("th", -32768, 32767)):
        v = np.asarray(d[k]).astype(np.float64)
        if not np.all((v >= lo) & (v <= hi) & (v == np.floor(v))): bad.append("range of " + k)
    p = np.asarray(d["pa"]).astype(np.float64); z = np.asarray(d["th"]).astype(np.float64)
    if np.any(p != p[:1]): bad.append("pa alike on all ranks")
    if np.any(z != z[:1]): bad.append("th alike on all ranks")
    if np.any(p[:, :, HB:] != 0): bad.append("zeros of pa")
    if np.any(z.reshape(-1, 8, 16)[:, :, HB:] != 0): bad.append("zeros of th")
    return bad
def reference(nx, bk, s0, pa, th):
    x = nx.astype(np.float32).astype(np.int64).reshape(N, 8, 16, V); b = bk.astype(np.int64).reshape(N, 8, 16, KB)
    s = s0.astype(np.float32).astype(np.int64).reshape(N, 8, 16, S)
    a = pa.astype(np.float32).astype(np.int64).reshape(N, 8, 16, 16)[..., :HB]; t = th.astype(np.int64).reshape(N, 8, 16)[..., :HB]
    lower = np.tri(S, S, -1) > 0
    src = (np.arange(N)[:, None] - 1 - np.arange(S)[None, :] // SB) % N
    for rnd in range(RO):
        h = hashes(s, a, t)
        cols = h[..., None] ^ np.arange(M)
        cand = np.take_along_axis(b, cols.reshape(N, 8, 1, S * M), 3).reshape(N, 8, 16, S, M)
        cand = np.ascontiguousarray(cand.transpose(0, 1, 3, 4, 2)).reshape(N, 8, S, 16 * M)
        w = np.take_along_axis(x, cand.reshape(N, 8, 1, S * 16 * M), 3).reshape(N, 8, 16, S, 16 * M)
        dist = np.add.reduce(np.abs(w - s[..., None]), axis=2)
        c = np.take_along_axis(cand, np.argmin(dist, axis=3)[..., None], 3)[..., 0]
        xc = np.take_along_axis(x, c[:, :, None, :], 3)
        x1 = xc + np.clip(s - xc, -CL, CL); h1 = hashes(x1, a, t)
        same = (c[..., :, None] == c[..., None, :]) | (h1[..., :, None] == h1[..., None, :])
        stand = ~np.any(same & lower, axis=3)
        s1 = (s + xc) & 255
        for r in range(N):
            for g in range(8):
                k = np.flatnonzero(stand[r, g]); ck = c[r, g, k]
                x[r, g][:, ck] = x1[r, g][:, k]
                b[r, g, (ck + k) & 15, h1[r, g, k]] = ck
        s = np.take_along_axis(s1, src[:, None, None, :], 0)
    return {"ys": s.reshape(N, 128, S).astype(np.float32), "yb": b.reshape(N, 128, KB).astype(np.float32)}

from concourse.bass import DstId, RemoteDMATransfer
from concourse.mybir import AluOpType, AxisListType, ActivationFunctionType

NR, NV, NB, NS, RO = 8, 4096, 2048, 112, 3
BIG = 8192.0
HALF = [(0, 4), (4, 3)]
CH = [[(9, 16, "S"), (0, 5, "R"), (5, 9, "R")],
      [(12, 16, "S"), (0, 4, "A"), (4, 8, "A"), (8, 10, "A"), (10, 12, "R")]]
CYC, PEC, GA, SCAT, LAT, FLY, BW, NEAR = 1.04e-3, 0.55e-3, 1.56, 3.5, 0.08, 4.5, 300.0e3, 0.1

F32, BF, I32, U16, F16 = "float32", "bfloat16", "int32", "uint16", "float16"


def _sb(n, d):
    return ("sbuf", [128, n], d)


SCRATCH = {
    "nxs": _sb(NV + NS, BF), "bki": _sb(NB, I32), "bkf": _sb(NB + 128, F32),
    "land0": _sb(NS, BF), "land1": _sb(NS, BF), "land2": _sb(NS, BF), "land3": _sb(NS, F32),
    "snd0": _sb(NS, BF), "snd1": _sb(NS, BF), "snd2": _sb(NS, F32),
    "pas": _sb(16, BF), "thi": _sb(1, I32), "pint": _sb(4, I32), "pf": _sb(4, F32), "cols": _sb(8, F32),
    "ij": _sb(144, F32), "jg": _sb(128, F32), "kb": _sb(224, F32), "dm": _sb(8, F32), "ones": _sb(1024, BF),
    "plo": _sb(128, BF), "phi": _sb(224, BF), "ident": _sb(128, BF), "nident": _sb(128, BF), "i2": _sb(128, BF),
    "mtab": _sb(4112, BF), "g8": _sb(8, F32), "am": _sb(128, BF), "nam": _sb(128, BF),
    "w0": _sb(128, BF), "w1": _sb(128, BF), "wrow": _sb(16, F32), "wtmp": _sb(16, F32), "two": _sb(16, F32),
    "zero": _sb(16, F32), "b1": _sb(144, BF), "b2": _sb(144, BF), "bn": _sb(144, BF),
    "ex": _sb(1792, BF), "mask": _sb(128, BF), "mz": _sb(224, BF),
    "rst": _sb(128, F32), "d0": _sb(NS, F32), "bo": _sb(128, BF), "bo16": _sb(128, F16), "tri": _sb(128, BF),
    "gt": _sb(128, BF), "spare": _sb(8, F32),
    "sig": _sb(NS, BF), "st": _sb(256, BF), "srep": _sb(1792, BF), "t1": _sb(NS, BF),
    "hs": _sb(224, F32), "hoff": _sb(16, U16), "cand": _sb(224, U16), "candf": _sb(224, F32),
    "w": _sb(3584, BF), "ab": _sb(3584, BF), "ks": _sb(224, F32), "ki": _sb(8, I32), "kint": _sb(16, I32),
    "koff": _sb(16, U16), "dsel": _sb(NS, BF), "wrap": _sb(NS, BF), "ccol": _sb(NS, F32),
    "csel": _sb(NS, F16), "cl": _sb(NS, BF), "sg2": _sb(NS, BF), "cw": _sb(NS, F32),
    "cta": _sb(8, U16), "cb": _sb(NS, F32), "mb": _sb(NS, BF), "hw": _sb(NS, F32),
    "h2off": _sb(8, U16), "qn": _sb(NS, F32), "fs": _sb(NS, F32), "foff": _sb(16, U16), "xn": _sb(NS, BF),
    "drop": _sb(8, F32), "cd": _sb(8, F32), "ce": _sb(8, F32),
    "ec": ("sbuf", [128, 7, 128], BF), "eh": ("sbuf", [128, 7, 128], BF),
}
for _k in range(8):
    SCRATCH["pb%d" % _k] = ("psum", [128, 512], F32)

DMAS = ["d_s0", "d_pa", "d_th", "d_bk0", "d_bk1", "d_nx", "d_ys", "d_yb"]
SEMAPHORES = ["cP", "cV", "cS", "cG", "sent"] + DMAS + ["arr%d%d" % (r, h) for r in range(RO) for h in range(2)]


def rank_program(g, core, T, topo):
    rank = T.rank_of(core)
    if rank is None:
        return
    OP, AF = AluOpType, ActivationFunctionType
    ops = []
    phase = [0]

    def R(name, a=0, b=None, step=1, np_=128):
        if b is None:
            b = SCRATCH[name][1][1]
        if step == 1:
            return (T[name][0:np_, a:b], [(name, ((1 << (b - a)) - 1) << a)])
        m = 0
        for j in range(a, b, step):
            m |= 1 << j
        return (T[name][0:np_, a:b:step], [(name, m)])

    def R3(name, r, a, b):
        rows = range(7) if r is None else [r]
        m = 0
        for q in rows:
            m |= ((1 << (b - a)) - 1) << (128 * q + a)
        return (T[name][:, :, a:b] if r is None else T[name][:, r, a:b], [(name, m)])

    def IND(win, off):
        return (win[0].indirect(off[0]), win[1], off[1])

    def isap(x):
        return isinstance(x, tuple)

    def ap(x):
        return x[0] if isap(x) else x

    def size(x):
        return bin(x[1][0][1]).count("1") if len(x) == 2 else 16 * bin(x[2][0][1]).count("1")

    def two(x):
        return SCRATCH[x[1][0][0]][2] in (BF, U16, F16)

    def vcost(out, in_, per):
        if len(in_) > 2:
            return 0.06 + size(in_) * GA * CYC
        if len(out) > 2:
            return 0.06 + size(out) * SCAT * CYC
        return max(64, size(in_) * per) * CYC

    def add(eng, fn, cost, outs, ins, sem=None, val=0, after=(), grp=None, lag=0.0):
        rd, wr = [], []
        for x in ins:
            if isap(x):
                rd += x[1] + (x[2] if len(x) > 2 else [])
        for x in outs:
            wr += x[1]
            rd += x[2] if len(x) > 2 else []
        ops.append({"eng": eng, "fn": fn, "cost": cost, "rd": rd, "wr": wr, "sem": sem, "val": val,
                    "after": list(after), "grp": grp, "lag": lag, "stop": False, "phase": phase[0]})
        return len(ops) - 1

    group = {}

    def mm(out, lhsT, rhs, start, after=()):
        bank = out[1][0][0]
        if start:
            group[bank] = len(ops)
        me = len(ops)
        return add("P", lambda: g.tensor.matmul(out[0], lhsT[0], rhs[0], start, ops[me]["stop"]),
                   max(64, size(rhs)) * PEC, [out], [lhsT, rhs], after=after, grp=group[bank])

    def cp(out, in_):
        add("V", lambda: g.vector.tensor_copy(out[0], in_[0]),
            vcost(out, in_, 0.5 if two(out) and two(in_) else 1), [out], [in_])

    def tt(out, a, b, op):
        add("V", lambda: g.vector.tensor_tensor(out[0], a[0], b[0], op), vcost(out, a, 2), [out], [a, b])

    def ts(out, a, s1, op0, s2=None, op1=None):
        c = vcost(out, a, 0.5 if two(out) and two(a) else 1)
        if op1 is None:
            add("V", lambda: g.vector.tensor_scalar(out[0], a[0], ap(s1), None, op0), c, [out], [a, s1])
        else:
            add("V", lambda: g.vector.tensor_scalar(out[0], a[0], ap(s1), ap(s2), op0, op1), c, [out], [a, s1, s2])

    def scan(out, d0, d1, init, op0, op1):
        add("V", lambda: g.vector.tensor_tensor_scan(out[0], d0[0], d1[0], init, op0, op1), vcost(out, d0, 1),
            [out], [d0, d1])

    def mset(out, v):
        add("V", lambda: g.vector.memset(out[0], v), vcost(out, out, 0.5 if two(out) else 1), [out], [])

    def act(out, in_, f, bias=0.0, scale=1.0):
        add("S", lambda: g.scalar.activation(out[0], in_[0], f, bias=ap(bias), scale=scale),
            0.08 + size(in_) * CYC * (GA if len(in_) > 2 else 1), [out], [in_, bias])

    def iota(out, pat, base, ch, small):
        c = 0.16 + 2 * size(out) * CYC
        if small:
            add("G", lambda: g.iota(out[0], pat, base, ch, allow_small_or_imprecise_dtypes=True), c, [out], [])
        else:
            add("G", lambda: g.iota(out[0], pat, base, ch), c, [out], [])

    def asel(out, in_, pat, op, base, ch):
        add("G", lambda: g.affine_select(out[0], in_[0], pat, op, 0.0, base, ch), 0.2 + 2 * size(out) * CYC,
            [out], [in_])

    busy = [2.0]

    def load(sem, out, src, nbytes):
        busy[0] += nbytes / BW
        prev = [i for i, o in enumerate(ops) if o["eng"] == "Y"][-1:]
        add("Y", lambda: g.sync.dma_start(out[0], src), 0.05, [out], [], sem, 16, after=prev, lag=busy[0])

    load("d_s0", R("land0"), T.s0[:], 0)
    load("d_pa", R("pas"), T.pa[:], 0)
    load("d_bk0", R("bki", 0, 1024), T.bk[:, 0:1024], 1 << 19)
    load("d_bk1", R("bki", 1024, 2048), T.bk[:, 1024:2048], 1 << 19)
    load("d_nx", R("nxs", 0, NV), T.nx[:], 1 << 20)
    add("G", lambda: g.dma_start(T.thi[:], T.th[:], allow_slow_non_contiguous=True), 1.0, [R("thi")], [], "d_th", 16,
        lag=2.0)

    iota(R("pint", 0, 1), [[0, 1]], 0, 1, False)
    iota(R("ij"), [[1, 144]], 0, 0, True)
    iota(R("jg"), [[1, 8], [0, 16]], 0, 0, True)
    phase[0] = 1
    iota(R("plo"), [[0, 8], [1, 16]], 0, 0, True)
    iota(R("dm"), [[16, 8]], 2048, 0, True)
    mset(R("ones"), 1.0)
    for b0, nb in HALF:
        iota(R("kb", 32 * b0, 32 * (b0 + nb)), [[256 * nb, 2], [16, nb], [0, 16]], 512 * b0, 0, True)
        asel(R("ex", 256 * b0, 256 * (b0 + nb)), R("ones", 0, 256 * nb), [[1, 16], [16, nb], [0, 16]], OP.is_equal,
             0, -1)
    mset(R("kint", 7, 8), 0)
    mset(R("two"), 2.0)
    mset(R("zero"), 0.0)
    mset(R("rst"), 0.0)
    mset(R("wrow", 11, 12), -1024.0)
    mset(R("wrow", 12, 13), 0.5)
    mset(R("wrow", 13, 16), 0.0)
    mset(R("d0"), -1.0)
    mset(R("mz", 112, 224), 0.0)
    mset(R("nxs", NV, NV + NS), 0.0)
    mset(R("bkf", NB, NB + 128), 0.0)
    mset(R("rst", 0, 128, 16), 3.0e7)
    scan(R("wrow", 0, 11), R("two", 0, 11), R("zero", 0, 11), 0.25, OP.mult, OP.add)
    ts(R("pint", 1, 2), R("pint", 0, 1), 15, OP.bitwise_and)
    ts(R("pint", 2, 3), R("pint", 0, 1), 4, OP.logical_shift_right)
    cp(R("pf", 0, 3), R("pint", 0, 3))
    pcol, acol, gcol = R("pf", 0, 1), R("pf", 1, 2), R("pf", 2, 3)
    ts(R("mtab", 0, 16), R("ij", 0, 16), acol, OP.is_equal)
    n = 16
    while n < 1024:
        cp(R("mtab", n, 2 * n), R("mtab", 0, n))
        n *= 2
    cp(R("mtab", 1024, 2048), R("mtab", 0, 1024))
    for n in range(2048, 4096, 256):
        act(R("mtab", n, n + 256), R("mtab", 0, 256), AF.Identity)
    act(R("mtab", 4096, 4112), R("mtab", 0, 16), AF.Identity)
    ts(R("g8"), R("ij", 0, 8), gcol, OP.is_equal)
    ts(R("ident"), R("ij", 0, 128), pcol, OP.is_equal)
    tt(R("wtmp"), R("wrow"), R("mtab", 0, 16), OP.mult)
    ts(R("cols", 0, 1), gcol, 16.0, OP.mult, 15.0, OP.add)
    add("V", lambda: g.vector.tensor_reduce(T.cols[:, 3:4], T.wtmp[:], AxisListType.X, OP.add), 0.07,
        [R("cols", 3, 4)], [R("wtmp")])
    tt(R("cols", 4, 5), R("cols", 3, 4), R("mtab", 0, 1), OP.subtract)
    ts(R("cols", 2, 3), acol, 2048.0, OP.add)
    for h, (b0, nb) in enumerate(HALF):
        ts(R("cols", 6 + h, 7 + h), acol, 16.0 * nb, OP.mult)
        act(R("phi", 32 * b0, 32 * (b0 + nb)), R("kb", 32 * b0, 32 * (b0 + nb)), AF.Identity, R("cols", 6 + h, 7 + h))
    for q in range(8):
        ts(R("am", 16 * q, 16 * q + 16), R("pas"), R("g8", q, q + 1), OP.mult)
    ts(R("w0"), R("jg"), gcol, OP.is_equal, R("cols", 3, 4), OP.mult)
    ts(R("w1"), R("jg"), gcol, OP.is_equal, R("cols", 4, 5), OP.mult)
    ts(R("cols", 5, 6), R("thi"), -1.0, OP.mult, -0.5, OP.add)
    sbias = R("cols", 5, 6)
    act(R("mask"), R("mtab", 0, 128), AF.Identity, BIG, -BIG)
    act(R("nident"), R("ident"), AF.Identity, 0.0, -1.0)
    act(R("i2"), R("ident"), AF.Identity, 0.0, 2.0)
    ts(R("b1"), R("ij"), R("cols", 0, 1), OP.is_equal, 4096.0, OP.mult)
    ts(R("bo16"), R("jg"), gcol, OP.is_equal)
    ts(R("gt"), R("plo"), acol, OP.is_gt)
    ts(R("bo"), R("jg"), gcol, OP.is_equal, BIG, OP.mult)
    tt(R("tri"), R("gt"), R("bo"), OP.mult)
    act(R("nam"), R("am"), AF.Identity, 0.0, -1.0)
    act(R("b2"), R("b1"), AF.Identity, 0.0, 2.0)
    act(R("bn"), R("b1"), AF.Identity, 0.0, -1.0)
    act(R("d0", 0, NS, 16), R("dm", 0, 7), AF.Identity, acol)
    act(R("spare"), R("dm"), AF.Identity, acol)
    act(R("mz", 0, 112), R("mtab", 0, 112), AF.Identity, BIG, -BIG)
    cp(R("bkf", 0, 1024), R("bki", 0, 1024))
    cp(R("bkf", 1024, 2048), R("bki", 1024, 2048))

    ident, nident = R("ident"), R("nident")
    nxw, bkw = R("nxs", 0, NV), R("bkf", 0, NB)
    SRB = [["pb2", "pb0"], ["pb4", "pb7"]]

    def first_s(h):
        return min([c[0] for c in CH[h] if c[2] == "S"] + [16])

    def hash_front(r, h):
        b0, nb = HALF[h]
        s, t0, nt = "land%d" % r, 16 * b0, 16 * nb
        st = R("st", 128 * h, 128 * h + 128, 1, nt)
        mm(R("pb6", 0, 2 * nt), ident, R("mask", 0, 2 * nt), True)
        for b in range(nb):
            mm(R("pb5", b, nt, nb), R("am"), R(s, t0 + 16 * b, t0 + 16 * b + 16), True)
        mm(R("pb5", 128, 256, 1, nt), R(s, t0, t0 + nt), ident, True)
        act(R("sig", t0, t0 + nt), R("pb5", 0, nt), AF.Sign, sbias)
        act(st, R("pb5", 128, 256, 1, nt), AF.Identity)
        mm(R("pb6", 0, nt), R("w0"), R("sig", t0, t0 + nt), False)
        mm(R("pb6", nt, 2 * nt), R("w1"), R("sig", t0, t0 + nt), False)
        scan(R("hs", 2 * t0, 2 * t0 + 2 * nt), R("rst", 0, 2 * nt), R("pb6", 0, 2 * nt), 0.0, OP.add, OP.min)
        cp(R("hoff", 2 * b0, 2 * b0 + 2 * nb), R("hs", 2 * t0 + 15, 2 * t0 + 2 * nt, 16))
        phase[0] += 2 * h
        cut = [0, min(8, first_s(h)) * nt, first_s(h) * nt]
        for n in range(2):
            lo, hi = 16 * t0 + cut[n], 16 * t0 + cut[n + 1]
            if hi > lo:
                mm(R(SRB[h][n], 0, hi - lo), st, R("ex", lo, hi, 1, nt), True)
                act(R("srep", lo, hi), R(SRB[h][n], 0, hi - lo), AF.Identity)
        asel(R("t1", t0, t0 + nt), R(s, t0, t0 + nt), [[0, nb], [1, 16]], OP.is_ge, -first_s(h), 0)

    def search(h, late):
        b0, nb = HALF[h]
        t0, nt = 16 * b0, 16 * nb
        st = R("st", 128 * h, 128 * h + 128, 1, nt)
        kbank = "pb%d" % h
        hoff = R("hoff", 2 * b0, 2 * b0 + 2 * nb)
        cp(R("cand", 2 * t0, 2 * t0 + 2 * nt), IND(bkw, hoff))
        was = phase[0]
        phase[0] = late
        act(R("candf", 2 * t0, 2 * t0 + 2 * nt), IND(bkw, hoff), AF.Identity)
        phase[0] = was
        mm(R(kbank, 0, 2 * nt), ident, R("phi", 2 * t0, 2 * t0 + 2 * nt), True)
        mm(R(kbank, 0, 2 * nt), ident, R("plo", 0, 2 * nt), False)
        for a0, a1, mode in CH[h]:
            for k in range(2):
                base = 32 * t0 + 16 * nt * k
                lo, hi = base + nt * a0, base + nt * a1
                src = IND(nxw, R("cand", lo // 16, hi // 16))

                def key(a, tab, buf, after=()):
                    return mm(R(kbank, nt * k, nt * k + nt), R(tab, 15 - a, 143 - a),
                              R(buf, base + nt * a, base + nt * a + nt), False, after)

                if mode == "S":
                    bank = R("pb%d" % (2 + k), 0, hi - lo)
                    act(R("w", lo, hi), src, AF.Identity)
                    mm(bank, st, R("ex", 16 * t0 + nt * a0, 16 * t0 + nt * a1, 1, nt), True)
                    mm(bank, nident, R("w", lo, hi), False)
                    act(R("ab", lo, hi), bank, AF.Abs)
                else:
                    tt(R("w", lo, hi), src, R("srep", 16 * t0 + nt * a0, 16 * t0 + nt * a1), OP.subtract)
                    if mode == "A":
                        act(R("ab", lo, hi), R("w", lo, hi), AF.Abs)
                    else:
                        ts(R("ab", lo, hi), R("w", lo, hi), 0.0, OP.max)
                for a in range(a0, a1):
                    if mode == "R":
                        key(a, "b2", "ab", [key(a, "bn", "w")])
                    else:
                        key(a, "b1", "ab")

    total = [0]

    def send(r, h):
        b0, nb = HALF[h]
        src, dst = "snd%d" % r, "land%d" % (r + 1)
        sem = "arr%d%d" % (r, h)

        def share(a, b):
            per = 1
            while 2 * per * nb <= len(topo.engines(a, b)):
                per *= 2
            return per

        def fn():
            trs = []
            for j in range(nb):
                b = b0 + j
                peer = T.cores[(rank + 1 + b) % NR]
                rid, pid, _ = topo.addr(peer)
                per = share(core, peer)
                m = 0
                for e in topo.engines(core, peer)[per * j:per * j + per]:
                    m |= 1 << e
                trs.append(RemoteDMATransfer(dst_ids=[DstId(rid=rid, pnc=pid)], dma_engine_mask=m,
                                             remote_sem=T.sem[sem], src=T[src][:, 16 * b:16 * b + 16],
                                             dst=T[dst][:, 16 * b:16 * b + 16]))
            return g.remote_dma_fused(trs, local_sem=T.sem["sent"])

        i = add("G", fn, 0.3, [], [R(src, 16 * b0, 16 * (b0 + nb))], "remote", 0)
        got = 0
        for b in range(b0, b0 + nb):
            got += share(T.cores[(rank - 1 - b) % NR], core)
            total[0] += share(core, T.cores[(rank + 1 + b) % NR])
        add("X", None, 0.0, [R(dst, 16 * b0, 16 * (b0 + nb))], [], sem, got, after=[i], lag=FLY)

    def argmin(r, h):
        b0, nb = HALF[h]
        s, t0, nt = "land%d" % r, 16 * b0, 16 * nb
        kbank = "pb%d" % h
        scan(R("ks", 2 * t0, 2 * t0 + 2 * nt), R("rst", 0, 2 * nt), R(kbank, 0, 2 * nt), 0.0, OP.add, OP.min)
        tt(R("ki", b0, b0 + nb), R("ks", 2 * t0 + 15, 2 * t0 + nt, 16), R("ks", 2 * t0 + nt + 15, 2 * t0 + 2 * nt, 16),
           OP.min)
        ts(R("kint", b0, b0 + nb), R("ki", b0, b0 + nb), 4095, OP.bitwise_and)
        if h:
            ts(R("kint", 8, 15), R("ki", 0, 7), 4095, OP.bitwise_and, 4, OP.logical_shift_right)
        cp(R("koff", b0, 15 if h else nb), R("kint", b0, 15 if h else nb))
        tt(R("dsel", t0, t0 + nt), IND(R("w", 0, 32 * (t0 + nt)), R("koff", b0, b0 + nb)), R("t1", t0, t0 + nt),
           OP.subtract)
        mm(R(kbank, 0, nt), R("i2"), R(s, t0, t0 + nt), True)
        mm(R(kbank, 0, nt), ident, R("dsel", t0, t0 + nt), False)
        ts(R("wrap", t0, t0 + nt), R(kbank, 0, nt), 256.0, OP.is_ge, -256.0, OP.mult)
        mm(R(kbank, 0, nt), R("i2"), R(s, t0, t0 + nt), True)
        mm(R(kbank, 0, nt), ident, R("dsel", t0, t0 + nt), False)
        mm(R(kbank, 0, nt), ident, R("wrap", t0, t0 + nt), False)
        act(R("snd%d" % r, t0, t0 + nt), R(kbank, 0, nt), AF.Identity)
        send(r, h)

    def earlier(name, rows, wrapped):
        for b in range(7):
            ts(R3(name, b, 0, NS - 16 * b), rows(16 * b), R(wrapped, 16 * b + 15, 16 * b + 16), OP.is_equal)
            if b < 6:
                mm(R("pb7", 16 * b + 16, NS), R("bo"), R3(name, b, 16, NS - 16 * b), False)
        mm(R("pb7", 0, NS), R("tri"), R3(name, None, 0, 16), False)

    def update(r):
        last = r == RO - 1
        s = "land%d" % r
        mm(R("pb7", 0, NS), ident, R("mask", 0, NS), True)
        mm(R("pb4", 0, 224), ident, R("mz"), True)
        mm(R("pb2", 0, NS), ident, R("mask", 0, NS), True)
        mm(R("pb5", 0, NS), R("am"), R(s), True)
        act(R("ccol"), IND(R("candf"), R("koff", 8, 15)), AF.Identity, -2048.0)
        ts(R("cl"), R("dsel"), -16.0, OP.max, 16.0, OP.min)
        tt(R("csel"), IND(R("mtab"), R("koff", 0, 7)), R("ccol"), OP.mult)
        mm(R("pb5", 0, NS), R("am"), R("dsel"), False)
        mm(R("pb5", 0, NS), R("nam"), R("cl"), False)
        act(R("sg2"), R("pb5", 0, NS), AF.Sign, sbias)
        mm(R("pb2", 0, NS), R("bo16"), R("csel"), False)
        mm(R("pb3", 0, NS), R("bo16"), R("csel"), True)
        mm(R("pb1", 0, NS), R("bo16"), R("csel"), True)
        scan(R("cw"), R("rst", 0, NS), R("pb2", 0, NS), 0.0, OP.add, OP.min)
        ts(R("cta", 0, 7), R("cw", 15, NS, 16), R("cols", 2, 3), OP.add)
        mm(R("pb4", 0, NS), R("w0"), R("sg2"), False)
        mm(R("pb4", NS, 224), R("w0"), R("sg2"), False)
        mm(R("pb7", 0, NS), R("w0"), R("sg2"), False)
        act(R("mb"), IND(R("mtab"), R("cta", 0, 7)), AF.Identity, 0.0, BIG)
        mm(R("pb1", 0, NS), ident, R("mb"), False)
        act(R("cb"), R("pb1", 0, NS), AF.Identity, 2048.0 - BIG)
        earlier("ec", lambda t: R("pb3", t, NS), "cw")
        if not last:
            mm(R("pb0", 0, NS), ident, R(s), True)
            mm(R("pb0", 0, NS), ident, R("dsel"), False)
            mm(R("pb0", 0, NS), nident, R("cl"), False)
            act(R("xn"), R("pb0", 0, NS), AF.Identity)
        scan(R("hw"), R("rst", 0, NS), R("pb4", 0, NS), 0.0, OP.add, OP.min)
        cp(R("h2off", 0, 7), R("hw", 15, NS, 16))
        earlier("eh", lambda t: R("pb4", NS + t, 224), "hw")
        tt(R("qn"), IND(bkw, R("h2off", 0, 7)), R("mb"), OP.subtract)
        scan(R("fs"), R("d0"), R("pb7", 0, NS), 0.0, OP.max, OP.min)
        cp(R("foff", 0, 7), R("fs", 15, NS, 16))
        if not last:
            ts(R("drop", 0, 7), R("fs", 15, NS, 16), 2048.0, OP.is_ge, BIG, OP.mult)
            tt(R("cd", 0, 7), R("drop", 0, 7), R("cw", 15, NS, 16), OP.add)
            tt(R("ce", 0, 7), R("cd", 0, 7), R("spare", 0, 7), OP.min)
            ts(R("foff", 8, 15), R("ce", 0, 7), 2048.0, OP.add)
            hash_front(r + 1, 0)
        tt(IND(R("bkf"), R("foff", 0, 7)), R("qn"), R("cb"), OP.max)
        if not last:
            cp(IND(R("nxs"), R("foff", 8, 15)), R("xn"))

    hash_front(0, 0)
    for r in range(RO):
        phase[0] = 10 * r + 1
        hash_front(r, 1)
        phase[0] = 10 * r + 2
        search(0, 10 * r + 4)
        argmin(r, 0)
        phase[0] = 10 * r + 3
        search(1, 10 * r + 4)
        argmin(r, 1)
        phase[0] = 10 * r + 4
        update(r)
    add("S", lambda: g.scalar.dma_start(T.ys[:], T.land3[:]), 0.05, [], [R("land3")], "d_ys", 16, lag=2.0)
    add("Y", lambda: g.sync.dma_start(T.yb[:], bkw[0]), 0.05, [], [bkw], "d_yb", 16, lag=5.0)

    hist = {}
    hard, soft = [], []
    for i, o in enumerate(ops):
        d, e = set(), set(o["after"])
        acc = [(n, m, False) for n, m in o["rd"]] + [(n, m, True) for n, m in o["wr"]]
        for n, m, w in acc:
            psum = SCRATCH[n][0] == "psum"
            for j, m2, w2 in hist.get(n, []):
                e2 = ops[j]["eng"]
                if e2 == "P" and o["eng"] == "P":
                    if psum and (ops[j]["grp"] != o["grp"] or j == o["grp"]):
                        e.add(j)
                elif (psum and e2 != o["eng"]) or ((m & m2) and (w or w2)):
                    d.add(j)
        for n, m, w in acc:
            hist.setdefault(n, []).append((i, m, w))
        hard.append(d)
        soft.append(e)

    nop = len(ops)
    succ = [[] for _ in ops]
    for i in range(nop):
        for j in hard[i] | soft[i]:
            succ[j].append(i)
    way = [0.0] * nop
    for i in range(nop - 1, -1, -1):
        way[i] = ops[i]["cost"] + ops[i]["lag"] + max([way[k] + LAT for k in succ[i]] + [0.0])
    grace = [NEAR if o["phase"] % 10 == 2 and o["eng"] in "VS" else 0.0 for o in ops]
    left = [len(hard[i] | soft[i]) for i in range(nop)]
    ready = [0.0] * nop
    free = {}
    pool = [i for i in range(nop) if left[i] == 0]
    order = []
    while pool:
        st = {i: max(ready[i], free.get(ops[i]["eng"], 0.0)) for i in pool}
        i0 = min(pool, key=lambda i: (st[i], -way[i], i))
        near = [i for i in pool if ops[i]["eng"] == ops[i0]["eng"] and st[i] <= st[i0] + grace[i]]
        i = min(near, key=lambda i: (ops[i]["phase"], -way[i], i))
        pool.remove(i)
        order.append(i)
        end = st[i] + ops[i]["cost"]
        if ops[i]["eng"] != "X":
            free[ops[i]["eng"]] = end
        for k in succ[i]:
            ready[k] = max(ready[k], end + ops[i]["lag"] + LAT if i in hard[k] else end)
            left[k] -= 1
            if left[k] == 0:
                pool.append(k)
    place = {i: n for n, i in enumerate(order)}
    closer = {}
    for i in order:
        if ops[i]["grp"] is not None:
            closer[ops[i]["grp"]] = i
    for i in closer.values():
        ops[i]["stop"] = True

    waits = []
    need = set()
    for i in range(nop):
        last = {}
        for j in (hard[i] if ops[i]["eng"] != "X" else []):
            k = ops[j]["sem"] or ops[j]["eng"]
            if k not in last or place[j] > place[last[k]]:
                last[k] = j
        waits.append(sorted(last.values()))
        need.update(last.values())
    cnt = {"P": 0, "V": 0, "S": 0, "G": 0}
    for i in order:
        o = ops[i]
        if o["sem"] is None and i in need:
            cnt[o["eng"]] += 1
            o["sem"], o["val"], o["inc"] = "c" + o["eng"], cnt[o["eng"]], 1
        else:
            o["inc"] = 16 if o["sem"] in DMAS else 0
    Q = {"P": g.tensor, "V": g.vector, "S": g.scalar, "G": g, "Y": g.sync}
    seen = {}
    for i in order:
        o = ops[i]
        e = o["eng"]
        if e == "X":
            continue
        for j in waits[i]:
            sem, val = ops[j]["sem"], ops[j]["val"]
            if seen.get((e, sem), 0) < val:
                seen[(e, sem)] = val
                Q[e].wait_ge(T.sem[sem], val)
        ins = o["fn"]()
        if o["inc"]:
            ins.then_inc(T.sem[o["sem"]], o["inc"])
    for e in cnt:
        if cnt[e]:
            g.wait_ge(T.sem["c" + e], cnt[e])
    for o in ops:
        if o["eng"] == "X" or o["sem"] in DMAS:
            g.wait_ge(T.sem[o["sem"]], o["val"])
    g.wait_ge(T.sem["sent"], total[0])
